import numpy as np
import ml_dtypes


def mxq(x, axis, fmt="e4m3"):
    dtype, down = {"e4m3": (ml_dtypes.float8_e4m3fn, 7), "e5m2": (ml_dtypes.float8_e5m2, 14)}[fmt]
    v = np.moveaxis(np.asarray(x, np.float32).astype(ml_dtypes.bfloat16).astype(np.float64), axis, -1)
    blocks = v.reshape(v.shape[:-1] + (-1, 32))
    amax = np.abs(blocks).max(-1, keepdims=True)
    byte = np.maximum(np.where(amax > 0, np.frexp(amax)[1] - 1 + 127, 0) - down, 1)
    scale = np.exp2(byte - 127.0)
    codes = (blocks / scale).astype(np.float32).astype(dtype).astype(np.float64)
    return np.moveaxis((codes * scale).reshape(v.shape), -1, axis)


WIDE = False


def mx_kscale(k):
    if not WIDE:
        return np.ones(k)
    levels = np.array([10, -10, 5, -5, 0])
    if k % 512:
        return np.exp2(np.random.permutation(np.resize(levels, k // 32))).repeat(32)
    a = np.empty((k // 512, 16))
    for p in range(k // 512):
        a[p, :8] = np.random.permutation(np.resize(levels, 8))
        for g in range(8):
            far = levels[np.abs(levels - a[p, g]) >= 10]
            a[p, g + 8] = far[np.random.randint(len(far))]
    return np.exp2(a.ravel()).repeat(32)


def f64(x):
    return np.asarray(x).astype(np.float64)


def striped(idx):
    return np.tile(np.asarray(idx).reshape(-1, 16).T, (8, 1)).astype(np.uint16)


def unstriped(offs):
    return offs[:16].T.reshape(-1).astype(np.int64)


def striped8(idx):
    return np.asarray(idx).reshape(8, -1, 16).transpose(0, 2, 1).reshape(128, -1).astype(np.uint16)


def unstriped8(offs):
    return offs.reshape(8, 16, -1).transpose(0, 2, 1).reshape(8, -1).astype(np.int64)


def pick8(x, idx, run):
    r = np.arange(len(x))
    return x[r[:, None], idx[r % (8 * run) // run]]


E2M1 = np.array([0.0, 0.5, 1.0, 1.5, 2.0, 3.0, 4.0, 6.0, -0.0, -0.5, -1.0, -1.5, -2.0, -3.0, -4.0, -6.0])


def pack_weight(w, fmt):
    k, n = w.shape
    w = f64(np.asarray(w, np.float32).astype(ml_dtypes.bfloat16)).reshape(k // 32, 32, n)
    amax = np.abs(w).max(1)
    if fmt == "e4m3":
        byte = np.frexp(amax)[1] - 1 + 127 - 7
    else:
        mant, ex = np.frexp(amax / 6.0)
        byte = np.where(mant > 0.5, ex, ex - 1) + 127
    byte = np.clip(np.where(amax > 0, byte, 1), 1, 254)
    scaled = (w * np.exp2(127.0 - byte)[:, None, :]).reshape(k, n).astype(np.float32)
    by_word = np.ascontiguousarray(scaled.reshape(k // 512, 128, 4, n).transpose(0, 1, 3, 2))
    if fmt == "e4m3":
        words = by_word.astype(ml_dtypes.float8_e4m3fn).view(np.uint8)
    else:
        c = by_word.astype(ml_dtypes.float4_e2m1fn).view(np.uint8) & 0xF
        words = (c[..., 0::2] | (c[..., 1::2] << 4)).reshape(k // 512, 128, 2 * n)
    return np.ascontiguousarray(words), np.ascontiguousarray(byte.astype(np.uint8).reshape(k // 512, 16, n))


def unpack_weight(words, scales, fmt):
    g, _, n = scales.shape
    words = np.ascontiguousarray(words).reshape(g, 128, n, -1)
    if fmt == "e4m3":
        vals = words.view(ml_dtypes.float8_e4m3fn).astype(np.float64)
    else:
        nib = np.empty((g, 128, n, 4), np.uint8)
        nib[..., 0::2] = words & 0xF
        nib[..., 1::2] = words >> 4
        vals = E2M1[nib]
    vals = vals * np.repeat(np.exp2(scales.astype(np.float64) - 127.0), 8, axis=1)[..., None]
    return vals.transpose(0, 1, 3, 2).reshape(g * 512, n)


def sgn(shape):
    return np.random.uniform(0.5, 2.0, shape) * np.where(np.random.standard_normal(shape) < 0, -1.0, 1.0)


K, J, R, T, F, O, N, U, E = 512, 1024, 512, 4096, 2048, 512, 256, 256, 1024


def setup_inputs():
    n = np.random.standard_normal
    idx = np.random.permutation(T)[:J]
    idx2 = np.stack([np.random.permutation(F)[:R] for _ in range(8)])
    idx3 = np.stack([np.random.permutation(F)[:R] for _ in range(8)])
    idx4 = np.random.permutation(J)[:O]
    idx5 = np.stack([np.random.permutation(J)[:O] for _ in range(8)])
    idx6 = np.stack([np.random.permutation(O)[:U] for _ in range(8)])
    idx7 = np.stack([np.random.permutation(E)[:U] for _ in range(8)])
    fk = mx_kscale(K)
    fr = mx_kscale(R)
    xtp = pack_weight(n((K, T)) * fk[:, None], "e4m3")
    wbp = pack_weight(n((R, N)) * 1 / np.sqrt(R) / fr[:, None], "e4m3")
    return {
        "xt_words": xtp[0],
        "xt_scales": xtp[1],
        "ua": (np.random.randint(-7, 8, (K, F)).astype(np.float64)).astype(np.float32),
        "ha": ((np.random.randint(10, 25, (K, 1)) / 1024.0) / fk[:, None]).astype(np.float32),
        "hb": ((np.random.randint(4, 13, (K, 1)) / 1024.0) / fk[:, None]).astype(np.float32),
        "sa": (np.random.uniform(0.5, 1.6, (R, 1)) * fr[:, None]).astype(np.float32),
        "sb": (np.random.uniform(0.5, 1.6, (R, 1)) * fr[:, None]).astype(np.float32),
        "wb_words": wbp[0],
        "wb_scales": wbp[1],
        "so": (sgn((N, 1))).astype(np.float32),
        "offs": striped(idx),
        "offs2": striped8(idx2),
        "offs3": striped8(idx3),
        "offs4": striped(idx4),
        "offs5": striped8(idx5),
        "offs6": striped8(idx6),
        "offs7": striped8(idx7),
    }


def reference(xt_words, xt_scales, ua, ha, hb, sa, sb, wb_words, wb_scales, so, offs, offs2, offs3, offs4, offs5, offs6, offs7):
    idx = unstriped(offs)
    idx2 = unstriped8(offs2)
    idx3 = unstriped8(offs3)
    idx4 = unstriped(offs4)
    idx5 = unstriped8(offs5)
    idx6 = unstriped8(offs6)
    idx7 = unstriped8(offs7)
    xtu = unpack_weight(xt_words, xt_scales, "e4m3")
    wbu = unpack_weight(wb_words, wb_scales, "e4m3")
    wc = pick8(f64(ua), idx2, 64) * f64(ha) + pick8(f64(ua), idx3, 64) * f64(hb)
    wcq = mxq(wc, 0, "e4m3")
    xtidxg = xtu[:, idx]
    a = wcq.T @ xtidxg
    hid = np.maximum(a[:, idx4] * f64(sa), pick8(a, idx5, 64) * f64(sb))
    hidq = mxq(hid, 0, "e4m3")
    p = wbu.T @ hidq
    m0 = pick8(p, idx6, 16) * f64(so)
    y = np.zeros((N, E))
    y[np.arange(N)[:, None], idx7[np.arange(N) % 128 // 16]] = m0
    return y

@@ -1,0 +1,203 @@
+from contextlib import ExitStack
+
+import concourse.mybir as mybir
+
+K, J, R, T, F, O, N, U, E = 512, 1024, 512, 4096, 2048, 512, 256, 256, 1024
+
+FLOPS = 2 * K * R * J + 2 * R * N * O
+
+F32 = mybir.dt.float32
+BF16 = mybir.dt.bfloat16
+I32 = mybir.dt.int32
+U32 = mybir.dt.uint32
+U16 = mybir.dt.uint16
+U8 = mybir.dt.uint8
+FP8X4 = mybir.dt.float8_e4m3fn_x4
+COPY = mybir.ActivationFunctionType.Copy
+ADD = mybir.AluOpType.add
+MAX = mybir.AluOpType.max
+
+P = 128
+PACK = 4
+BANK = 512
+LIST_ROWS = 16
+SLOT_PIECES = (512, 256, 256)
+PLACE_CHUNKS = (64, 128, 128, 128, 64)
+
+
+def runs(widths):
+    starts = [sum(widths[:i]) for i in range(len(widths))]
+    return [(start, start + width) for start, width in zip(starts, widths)]
+
+
+def entries(offsets, lo, hi):
+    return offsets[:, lo // LIST_ROWS : hi // LIST_ROWS]
+
+
+def tile_picked_tokens_refined_one_mixedpair_one_posted_kernel(
+    tc, xt_words, xt_scales, ua, ha, hb, sa, sb, wb_words, wb_scales, so,
+    offs, offs2, offs3, offs4, offs5, offs6, offs7, out,
+):
+    nc = tc.nc
+    with ExitStack() as ctx:
+        keep = ctx.enter_context(tc.tile_pool(name="keep", bufs=1))
+        ring = ctx.enter_context(tc.tile_pool(name="ring", bufs=2))
+        psum = ctx.enter_context(tc.psum_pool(name="psum", bufs=8))
+
+        def load_list(source, name):
+            tile = keep.tile(list(source.shape), U16, name=name)
+            nc.sync.dma_start(tile[:], source)
+            return tile
+
+        def load_dealt_column(queue, source, name):
+            tile = keep.tile([P, PACK], F32, name=name)
+            queue.dma_start(tile[:], source.rearrange("(p t) one -> p (t one)", t=PACK))
+            return tile
+
+        def load_code_rows(t):
+            tile = keep.tile([P, F], F32, name=f"ua_rows{t}")
+            nc.sync.dma_start(tile[:], ua.rearrange("(p t) f -> t p f", t=PACK)[t])
+            return tile
+
+        token_bytes = keep.tile([P, T], U8, name="token_bytes")
+        slot_scales = keep.tile([P, J], U8, name="slot_scales", align_bytes=64)
+        wb_plane = keep.tile([P, N], U8, name="wb_plane", align_bytes=64)
+        pages = [keep.tile([P, E], F32, name=f"page{n}") for n in range(N // P)]
+        nc.vector.memset(token_bytes[:].bitcast(I32), 0)
+        nc.vector.memset(slot_scales[:].bitcast(I32), 0)
+        nc.vector.memset(wb_plane[:].bitcast(I32), 0)
+        for page in pages:
+            nc.vector.memset(page[:], 0.0)
+
+        list2 = load_list(offs2, "list2")
+        ua_rows = [load_code_rows(0)]
+        nc.sync.dma_start(token_bytes[32:96:4, :].bitcast(I32), xt_scales[0].bitcast(I32))
+        ha_col = load_dealt_column(nc.scalar, ha, "ha_col")
+        hb_col = load_dealt_column(nc.scalar, hb, "hb_col")
+        list3 = load_list(offs3, "list3")
+        list1 = load_list(offs, "list1")
+        ua_rows.extend(load_code_rows(t) for t in range(1, PACK))
+        token_words = keep.tile([P, T], U32, name="token_words", tag="words", align_bytes=64)
+        nc.sync.dma_start(token_words[:].bitcast(I32), xt_words[0].rearrange("p c r -> p (c r)").bitcast(I32))
+        list5 = load_list(offs5, "list5")
+        sb_col = load_dealt_column(nc.sync, sb, "sb_col")
+        list4 = load_list(offs4, "list4")
+        sa_col = load_dealt_column(nc.sync, sa, "sa_col")
+        wb_codes = keep.tile([P, N], U32, name="wb_codes", align_bytes=64)
+        nc.sync.dma_start(wb_codes[:].bitcast(I32), wb_words[0].rearrange("p c r -> p (c r)").bitcast(I32))
+        for q in range(4):
+            nc.sync.dma_start(wb_plane[32 * q : 32 * q + 4, :].bitcast(I32), wb_scales[0, 4 * q : 4 * q + 4, :].bitcast(I32))
+        list6 = load_list(offs6, "list6")
+        list7 = load_list(offs7, "list7")
+        so_col = keep.tile([P, N // P], F32, name="so_col")
+        with nc.allow_non_contiguous_dma(reason="one value a partition for each block of 128 output features"):
+            nc.sync.dma_start(so_col[:], so.rearrange("(n p) one -> p (n one)", p=P))
+
+        picked_bytes = keep.tile([P, J], U8, name="picked_bytes")
+        nc.vector.tensor_copy(picked_bytes[:], token_bytes[:].indirect(list1[:]))
+        for q in range(4):
+            nc.gpsimd.dma_start(
+                slot_scales[32 * q : 32 * q + 4, :].bitcast(I32),
+                picked_bytes[32 + 16 * q : 48 + 16 * q : 4, :].bitcast(I32),
+            )
+
+        wc_rows = keep.tile([P, PACK, R], BF16, name="wc_rows")
+        for t in range(PACK):
+            coarse = keep.tile([P, R], F32, name=f"coarse{t}")
+            fine = keep.tile([P, R], F32, name=f"fine{t}")
+            nc.scalar.activation(coarse[:], ua_rows[t][:].indirect(list2[:]), COPY, scale=ha_col[:, t : t + 1])
+            nc.scalar.activation(fine[:], ua_rows[t][:].indirect(list3[:]), COPY, scale=hb_col[:, t : t + 1])
+            nc.vector.tensor_tensor(wc_rows[:, t, :], coarse[:], fine[:], ADD)
+
+        wc_dealt = wc_rows[:].rearrange("p t (c i s) -> p s c t i", i=2, s=PACK)
+        wc_grouped = []
+        for s in range(PACK):
+            grouped = keep.tile([P, P, PACK], BF16, name=f"wc_grouped{s}", align_bytes=64)
+            woven = grouped[:].rearrange("p (c i) t -> p c t i", i=2)
+            if s == 0:
+                nc.vector.tensor_copy(woven, wc_dealt[:, s])
+            else:
+                nc.scalar.copy(woven, wc_dealt[:, s])
+            wc_grouped.append(grouped)
+
+        def quantise_wc(s, codes):
+            plane = keep.tile([P, P], U8, name=f"wc_plane{s}", align_bytes=64)
+            nc.vector.quantize_mx(codes.bitcast(FP8X4), plane[:], wc_grouped[s][:].rearrange("p m t -> p (m t)"))
+            return codes, plane
+
+        first_codes = keep.tile([P, P], U32, name="first_codes", align_bytes=64)
+        wc_mx = [quantise_wc(0, first_codes[:])]
+
+        slot_words = keep.tile([P, J], U32, name="slot_words", align_bytes=64)
+        for lo, hi in runs(SLOT_PIECES):
+            nc.vector.tensor_copy(slot_words[:, lo:hi], token_words[:].indirect(entries(list1, lo, hi)))
+
+        other_codes = keep.tile([P, PACK - 1, P], U32, name="other_codes", tag="words", align_bytes=64)
+        wc_mx.extend(quantise_wc(s, other_codes[:, s - 1, :]) for s in range(1, PACK))
+
+        a_rows = []
+        for s, (codes, plane) in enumerate(wc_mx):
+            rows = keep.tile([P, J], F32, name=f"a_rows{s}")
+            for lo, hi in runs(SLOT_PIECES if s == 0 else (BANK, BANK)):
+                bank = psum.tile([P, BANK], F32, name="bank")
+                nc.tensor.matmul_mx(
+                    bank[:, : hi - lo],
+                    lhsT=codes.bitcast(FP8X4),
+                    lhsT_scale=plane[:],
+                    rhs=slot_words[:, lo:hi].bitcast(FP8X4),
+                    rhs_scale=slot_scales[:, lo:hi],
+                    start=True,
+                    stop=True,
+                )
+                if s == 0:
+                    nc.scalar.copy(rows[:, lo:hi], bank[:, : hi - lo])
+                else:
+                    nc.vector.tensor_copy(rows[:, lo:hi], bank[:, : hi - lo])
+            a_rows.append(rows)
+
+        second = keep.tile([P, PACK, O], F32, name="second")
+        for s in range(PACK):
+            nc.scalar.activation(second[:, s, :], a_rows[s][:].indirect(list5[:]), COPY, scale=sb_col[:, s : s + 1])
+
+        p_rows = [keep.tile([P, O], F32, name=f"p_rows{n}") for n in range(N // P)]
+        chunks = runs(PLACE_CHUNKS)
+        last_lo = chunks[-1][0]
+        early = [psum.tile([P, BANK], F32, name="bank") for n in range(N // P)]
+        late = [psum.tile([P, BANK], F32, name="bank") for n in range(N // P)]
+        for number, (lo, hi) in enumerate(chunks):
+            width = hi - lo
+            first = ring.tile([P, PACK, width], F32, name="first")
+            for s in range(PACK):
+                nc.scalar.activation(
+                    first[:, s, :], a_rows[s][:].indirect(entries(list4, lo, hi)), COPY, scale=sa_col[:, s : s + 1]
+                )
+            grouped = keep.tile([P, width, PACK], BF16, name=f"hid_grouped{number}", align_bytes=64)
+            nc.vector.tensor_tensor(
+                grouped[:].rearrange("p (c i) s -> p c s i", i=2),
+                first[:].rearrange("p s (c i) -> p c s i", i=2),
+                second[:, :, lo:hi].rearrange("p s (c i) -> p c s i", i=2),
+                MAX,
+            )
+            codes = keep.tile([P, width], U32, name=f"hid_codes{number}", align_bytes=64)
+            plane = keep.tile([P, width], U8, name=f"hid_plane{number}", align_bytes=64)
+            nc.vector.quantize_mx(codes[:].bitcast(FP8X4), plane[:], grouped[:].rearrange("p o s -> p (o s)"))
+            for n in range(N // P):
+                target = late[n][:, :width] if lo == last_lo else early[n][:, lo:hi]
+                nc.tensor.matmul_mx(
+                    target,
+                    lhsT=wb_codes[:, n * P : (n + 1) * P].bitcast(FP8X4),
+                    lhsT_scale=wb_plane[:, n * P : (n + 1) * P],
+                    rhs=codes[:].bitcast(FP8X4),
+                    rhs_scale=plane[:],
+                    start=True,
+                    stop=True,
+                )
+
+        for n in range(N // P):
+            empty = nc.scalar.copy if n == 0 else nc.vector.tensor_copy
+            empty(p_rows[n][:, :last_lo], early[n][:, :last_lo])
+            empty(p_rows[n][:, last_lo:], late[n][:, : O - last_lo])
+            ends = keep.tile([P, U], F32, name=f"ends{n}")
+            nc.scalar.activation(ends[:], p_rows[n][:].indirect(list6[:]), COPY, scale=so_col[:, n : n + 1])
+            nc.vector.tensor_copy(pages[n][:].indirect(list7[:]), ends[:])
+            nc.sync.dma_start(out[n * P : (n + 1) * P, :], pages[n][:])

@@ -22,7 +22,7 @@ PACK = 4
 BANK = 512
 LIST_ROWS = 16
 SLOT_PIECES = (512, 256, 256)
-PLACE_CHUNKS = (64, 128, 128, 128, 64)
+PLACE_CHUNKS = (64, 256, 128, 64)
 
 
 def runs(widths):
@@ -102,23 +102,24 @@ def tile_picked_tokens_refined_one_mixedpair_one_posted_kernel(
             )
 
         wc_rows = keep.tile([P, PACK, R], BF16, name="wc_rows")
+        wc_dealt = wc_rows[:].rearrange("p t (c i s) -> p s c t i", i=2, s=PACK)
+        wc_grouped = [keep.tile([P, P, PACK], BF16, name=f"wc_grouped{s}", align_bytes=64) for s in range(PACK)]
+        wc_woven = [grouped[:].rearrange("p (c i) t -> p c t i", i=2) for grouped in wc_grouped]
+        last = PACK - 1
         for t in range(PACK):
             coarse = keep.tile([P, R], F32, name=f"coarse{t}")
             fine = keep.tile([P, R], F32, name=f"fine{t}")
             nc.scalar.activation(coarse[:], ua_rows[t][:].indirect(list2[:]), COPY, scale=ha_col[:, t : t + 1])
             nc.scalar.activation(fine[:], ua_rows[t][:].indirect(list3[:]), COPY, scale=hb_col[:, t : t + 1])
-            nc.vector.tensor_tensor(wc_rows[:, t, :], coarse[:], fine[:], ADD)
-
-        wc_dealt = wc_rows[:].rearrange("p t (c i s) -> p s c t i", i=2, s=PACK)
-        wc_grouped = []
-        for s in range(PACK):
-            grouped = keep.tile([P, P, PACK], BF16, name=f"wc_grouped{s}", align_bytes=64)
-            woven = grouped[:].rearrange("p (c i) t -> p c t i", i=2)
-            if s == 0:
-                nc.vector.tensor_copy(woven, wc_dealt[:, s])
+            if t < last:
+                nc.vector.tensor_tensor(wc_rows[:, t, :], coarse[:], fine[:], ADD)
             else:
-                nc.scalar.copy(woven, wc_dealt[:, s])
-            wc_grouped.append(grouped)
+                nc.vector.tensor_copy(wc_woven[0][:, :, :last, :], wc_dealt[:, 0, :, :last, :])
+                by_block = [rows.rearrange("p (m s) -> p m s", s=PACK) for rows in (wc_rows[:, t, :], coarse[:], fine[:])]
+                nc.vector.tensor_tensor(wc_grouped[0][:, :, t], by_block[1][:, :, 0], by_block[2][:, :, 0], ADD)
+                nc.vector.tensor_tensor(by_block[0][:, :, 1:], by_block[1][:, :, 1:], by_block[2][:, :, 1:], ADD)
+        for s in range(1, PACK):
+            nc.scalar.copy(wc_woven[s], wc_dealt[:, s])
 
         def quantise_wc(s, codes):
             plane = keep.tile([P, P], U8, name=f"wc_plane{s}", align_bytes=64)
@@ -159,9 +160,8 @@ def tile_picked_tokens_refined_one_mixedpair_one_posted_kernel(
         for s in range(PACK):
             nc.scalar.activation(second[:, s, :], a_rows[s][:].indirect(list5[:]), COPY, scale=sb_col[:, s : s + 1])
 
-        p_rows = [keep.tile([P, O], F32, name=f"p_rows{n}") for n in range(N // P)]
         chunks = runs(PLACE_CHUNKS)
-        last_lo = chunks[-1][0]
+        last_lo = chunks[-2][0]
         early = [psum.tile([P, BANK], F32, name="bank") for n in range(N // P)]
         late = [psum.tile([P, BANK], F32, name="bank") for n in range(N // P)]
         for number, (lo, hi) in enumerate(chunks):
@@ -171,7 +171,7 @@ def tile_picked_tokens_refined_one_mixedpair_one_posted_kernel(
                 nc.scalar.activation(
                     first[:, s, :], a_rows[s][:].indirect(entries(list4, lo, hi)), COPY, scale=sa_col[:, s : s + 1]
                 )
-            grouped = keep.tile([P, width, PACK], BF16, name=f"hid_grouped{number}", align_bytes=64)
+            grouped = keep.tile([P, width, PACK], BF16, name=f"hid_grouped{number}", tag=f"hid{number}", align_bytes=64)
             nc.vector.tensor_tensor(
                 grouped[:].rearrange("p (c i) s -> p c s i", i=2),
                 first[:].rearrange("p s (c i) -> p c s i", i=2),
@@ -182,7 +182,7 @@ def tile_picked_tokens_refined_one_mixedpair_one_posted_kernel(
             plane = keep.tile([P, width], U8, name=f"hid_plane{number}", align_bytes=64)
             nc.vector.quantize_mx(codes[:].bitcast(FP8X4), plane[:], grouped[:].rearrange("p o s -> p (o s)"))
             for n in range(N // P):
-                target = late[n][:, :width] if lo == last_lo else early[n][:, lo:hi]
+                target = late[n][:, lo - last_lo : hi - last_lo] if lo >= last_lo else early[n][:, lo:hi]
                 nc.tensor.matmul_mx(
                     target,
                     lhsT=wb_codes[:, n * P : (n + 1) * P].bitcast(FP8X4),
@@ -193,6 +193,10 @@ def tile_picked_tokens_refined_one_mixedpair_one_posted_kernel(
                     stop=True,
                 )
 
+        p_rows = [
+            keep.tile([P, O], F32, name="p_rows0"),
+            keep.tile([P, O], F32, name="p_rows1", tag=f"hid{len(chunks) - 1}", align_bytes=64),
+        ]
         for n in range(N // P):
             empty = nc.scalar.copy if n == 0 else nc.vector.tensor_copy
             empty(p_rows[n][:, :last_lo], early[n][:, :last_lo])

@@ -59,6 +59,11 @@ def tile_picked_tokens_refined_one_mixedpair_one_posted_kernel(
             nc.sync.dma_start(tile[:], ua.rearrange("(p t) f -> t p f", t=PACK)[t])
             return tile
 
+        warm_in = keep.tile([P, 1], F32, name="warm_in")
+        warm_out = keep.tile([P, 1], F32, name="warm_out")
+        nc.vector.memset(warm_in[:], 0.0)
+        nc.scalar.activation(warm_out[:], warm_in[:], COPY)
+
         token_bytes = keep.tile([P, T], U8, name="token_bytes")
         slot_scales = keep.tile([P, J], U8, name="slot_scales", align_bytes=64)
         wb_plane = keep.tile([P, N], U8, name="wb_plane", align_bytes=64)

@@ -74,13 +74,13 @@ def tile_picked_tokens_refined_one_mixedpair_one_posted_kernel(
         for page in pages:
             nc.vector.memset(page[:], 0.0)
 
+        list1 = load_list(offs, "list1")
         list2 = load_list(offs2, "list2")
         ua_rows = [load_code_rows(0)]
-        nc.sync.dma_start(token_bytes[32:96:4, :].bitcast(I32), xt_scales[0].bitcast(I32))
         ha_col = load_dealt_column(nc.scalar, ha, "ha_col")
         hb_col = load_dealt_column(nc.scalar, hb, "hb_col")
+        nc.scalar.dma_start(token_bytes[32:96:4, :].bitcast(I32), xt_scales[0].bitcast(I32))
         list3 = load_list(offs3, "list3")
-        list1 = load_list(offs, "list1")
         ua_rows.extend(load_code_rows(t) for t in range(1, PACK))
         token_words = keep.tile([P, T], U32, name="token_words", tag="words", align_bytes=64)
         nc.sync.dma_start(token_words[:].bitcast(I32), xt_words[0].rearrange("p c r -> p (c r)").bitcast(I32))
@@ -177,12 +177,20 @@ def tile_picked_tokens_refined_one_mixedpair_one_posted_kernel(
                     first[:, s, :], a_rows[s][:].indirect(entries(list4, lo, hi)), COPY, scale=sa_col[:, s : s + 1]
                 )
             grouped = keep.tile([P, width, PACK], BF16, name=f"hid_grouped{number}", tag=f"hid{number}", align_bytes=64)
-            nc.vector.tensor_tensor(
-                grouped[:].rearrange("p (c i) s -> p c s i", i=2),
-                first[:].rearrange("p s (c i) -> p c s i", i=2),
-                second[:, :, lo:hi].rearrange("p s (c i) -> p c s i", i=2),
-                MAX,
-            )
+            if number < 2:
+                larger = keep.tile([P, PACK, width], BF16, name=f"larger{number}")
+                for rows in (slice(0, last), slice(last, PACK)):
+                    nc.vector.tensor_tensor(larger[:, rows, :], first[:, rows, :], second[:, rows, lo:hi], MAX)
+                nc.vector.tensor_copy(
+                    grouped[:].rearrange("p (c i) s -> p c s i", i=4), larger[:].rearrange("p s (c i) -> p c s i", i=4)
+                )
+            else:
+                nc.vector.tensor_tensor(
+                    grouped[:].rearrange("p (c i) s -> p c s i", i=2),
+                    first[:].rearrange("p s (c i) -> p c s i", i=2),
+                    second[:, :, lo:hi].rearrange("p s (c i) -> p c s i", i=2),
+                    MAX,
+                )
             codes = keep.tile([P, width], U32, name=f"hid_codes{number}", align_bytes=64)
             plane = keep.tile([P, width], U8, name=f"hid_plane{number}", align_bytes=64)
             nc.vector.quantize_mx(codes[:].bitcast(FP8X4), plane[:], grouped[:].rearrange("p o s -> p (o s)"))

@@ -84,6 +84,14 @@ def tile_picked_tokens_refined_one_mixedpair_one_posted_kernel(
         ua_rows.extend(load_code_rows(t) for t in range(1, PACK))
         token_words = keep.tile([P, T], U32, name="token_words", tag="words", align_bytes=64)
         nc.sync.dma_start(token_words[:].bitcast(I32), xt_words[0].rearrange("p c r -> p (c r)").bitcast(I32))
+        picked_bytes = keep.tile([P, J], U8, name="picked_bytes")
+        nc.vector.tensor_copy(picked_bytes[:], token_bytes[:].indirect(list1[:]))
+        for q in range(4):
+            nc.sync.dma_start(
+                slot_scales[32 * q : 32 * q + 4, :].bitcast(I32),
+                picked_bytes[32 + 16 * q : 48 + 16 * q : 4, :].bitcast(I32),
+            )
+
         list5 = load_list(offs5, "list5")
         sb_col = load_dealt_column(nc.sync, sb, "sb_col")
         list4 = load_list(offs4, "list4")
@@ -97,14 +105,6 @@ def tile_picked_tokens_refined_one_mixedpair_one_posted_kernel(
         so_col = keep.tile([P, N // P], F32, name="so_col")
         with nc.allow_non_contiguous_dma(reason="one value a partition for each block of 128 output features"):
             nc.sync.dma_start(so_col[:], so.rearrange("(n p) one -> p (n one)", p=P))
-
-        picked_bytes = keep.tile([P, J], U8, name="picked_bytes")
-        nc.vector.tensor_copy(picked_bytes[:], token_bytes[:].indirect(list1[:]))
-        for q in range(4):
-            nc.gpsimd.dma_start(
-                slot_scales[32 * q : 32 * q + 4, :].bitcast(I32),
-                picked_bytes[32 + 16 * q : 48 + 16 * q : 4, :].bitcast(I32),
-            )
 
         wc_rows = keep.tile([P, PACK, R], BF16, name="wc_rows")
         wc_dealt = wc_rows[:].rearrange("p t (c i s) -> p s c t i", i=2, s=PACK)

from contextlib import ExitStack

import concourse.mybir as mybir

K, J, R, T, F, O, N, U, E = 512, 1024, 512, 4096, 2048, 512, 256, 256, 1024

FLOPS = 2 * K * R * J + 2 * R * N * O

F32 = mybir.dt.float32
BF16 = mybir.dt.bfloat16
I32 = mybir.dt.int32
U32 = mybir.dt.uint32
U16 = mybir.dt.uint16
U8 = mybir.dt.uint8
FP8X4 = mybir.dt.float8_e4m3fn_x4
COPY = mybir.ActivationFunctionType.Copy
ADD = mybir.AluOpType.add
MAX = mybir.AluOpType.max

P = 128
PACK = 4
BANK = 512
LIST_ROWS = 16
SLOT_PIECES = (512, 256, 256)
PLACE_CHUNKS = (64, 256, 128, 64)


def runs(widths):
    starts = [sum(widths[:i]) for i in range(len(widths))]
    return [(start, start + width) for start, width in zip(starts, widths)]


def entries(offsets, lo, hi):
    return offsets[:, lo // LIST_ROWS : hi // LIST_ROWS]


def tile_picked_tokens_refined_one_mixedpair_one_posted_kernel(
    tc, xt_words, xt_scales, ua, ha, hb, sa, sb, wb_words, wb_scales, so,
    offs, offs2, offs3, offs4, offs5, offs6, offs7, out,
):
    nc = tc.nc
    with ExitStack() as ctx:
        keep = ctx.enter_context(tc.tile_pool(name="keep", bufs=1))
        ring = ctx.enter_context(tc.tile_pool(name="ring", bufs=2))
        psum = ctx.enter_context(tc.psum_pool(name="psum", bufs=8))

        def load_list(source, name):
            tile = keep.tile(list(source.shape), U16, name=name)
            nc.sync.dma_start(tile[:], source)
            return tile

        def load_dealt_column(queue, source, name):
            tile = keep.tile([P, PACK], F32, name=name)
            queue.dma_start(tile[:], source.rearrange("(p t) one -> p (t one)", t=PACK))
            return tile

        def load_code_rows(t):
            tile = keep.tile([P, F], F32, name=f"ua_rows{t}")
            nc.sync.dma_start(tile[:], ua.rearrange("(p t) f -> t p f", t=PACK)[t])
            return tile

        warm_in = keep.tile([P, 1], F32, name="warm_in")
        warm_out = keep.tile([P, 1], F32, name="warm_out")
        nc.vector.memset(warm_in[:], 0.0)
        nc.scalar.activation(warm_out[:], warm_in[:], COPY)

        token_bytes = keep.tile([P, T], U8, name="token_bytes")
        slot_scales = keep.tile([P, J], U8, name="slot_scales", align_bytes=64)
        wb_plane = keep.tile([P, N], U8, name="wb_plane", align_bytes=64)
        pages = [keep.tile([P, E], F32, name=f"page{n}") for n in range(N // P)]
        nc.vector.memset(token_bytes[:].bitcast(I32), 0)
        nc.vector.memset(slot_scales[:].bitcast(I32), 0)
        nc.vector.memset(wb_plane[:].bitcast(I32), 0)
        for page in pages:
            nc.vector.memset(page[:], 0.0)

        list1 = load_list(offs, "list1")
        list2 = load_list(offs2, "list2")
        ua_rows = [load_code_rows(0)]
        ha_col = load_dealt_column(nc.scalar, ha, "ha_col")
        hb_col = load_dealt_column(nc.scalar, hb, "hb_col")
        nc.scalar.dma_start(token_bytes[32:96:4, :].bitcast(I32), xt_scales[0].bitcast(I32))
        list3 = load_list(offs3, "list3")
        ua_rows.extend(load_code_rows(t) for t in range(1, PACK))
        token_words = keep.tile([P, T], U32, name="token_words", tag="words", align_bytes=64)
        nc.sync.dma_start(token_words[:].bitcast(I32), xt_words[0].rearrange("p c r -> p (c r)").bitcast(I32))
        picked_bytes = keep.tile([P, J], U8, name="picked_bytes")
        nc.vector.tensor_copy(picked_bytes[:], token_bytes[:].indirect(list1[:]))
        for q in range(4):
            nc.sync.dma_start(
                slot_scales[32 * q : 32 * q + 4, :].bitcast(I32),
                picked_bytes[32 + 16 * q : 48 + 16 * q : 4, :].bitcast(I32),
            )

        list5 = load_list(offs5, "list5")
        sb_col = load_dealt_column(nc.sync, sb, "sb_col")
        list4 = load_list(offs4, "list4")
        sa_col = load_dealt_column(nc.sync, sa, "sa_col")
        wb_codes = keep.tile([P, N], U32, name="wb_codes", align_bytes=64)
        nc.sync.dma_start(wb_codes[:].bitcast(I32), wb_words[0].rearrange("p c r -> p (c r)").bitcast(I32))
        for q in range(4):
            nc.sync.dma_start(wb_plane[32 * q : 32 * q + 4, :].bitcast(I32), wb_scales[0, 4 * q : 4 * q + 4, :].bitcast(I32))
        list6 = load_list(offs6, "list6")
        list7 = load_list(offs7, "list7")
        so_col = keep.tile([P, N // P], F32, name="so_col")
        with nc.allow_non_contiguous_dma(reason="one value a partition for each block of 128 output features"):
            nc.sync.dma_start(so_col[:], so.rearrange("(n p) one -> p (n one)", p=P))

        wc_rows = keep.tile([P, PACK, R], BF16, name="wc_rows")
        wc_dealt = wc_rows[:].rearrange("p t (c i s) -> p s c t i", i=2, s=PACK)
        wc_grouped = [keep.tile([P, P, PACK], BF16, name=f"wc_grouped{s}", align_bytes=64) for s in range(PACK)]
        wc_woven = [grouped[:].rearrange("p (c i) t -> p c t i", i=2) for grouped in wc_grouped]
        last = PACK - 1
        for t in range(PACK):
            coarse = keep.tile([P, R], F32, name=f"coarse{t}")
            fine = keep.tile([P, R], F32, name=f"fine{t}")
            nc.scalar.activation(coarse[:], ua_rows[t][:].indirect(list2[:]), COPY, scale=ha_col[:, t : t + 1])
            nc.scalar.activation(fine[:], ua_rows[t][:].indirect(list3[:]), COPY, scale=hb_col[:, t : t + 1])
            if t < last:
                nc.vector.tensor_tensor(wc_rows[:, t, :], coarse[:], fine[:], ADD)
            else:
                nc.vector.tensor_copy(wc_woven[0][:, :, :last, :], wc_dealt[:, 0, :, :last, :])
                by_block = [rows.rearrange("p (m s) -> p m s", s=PACK) for rows in (wc_rows[:, t, :], coarse[:], fine[:])]
                nc.vector.tensor_tensor(wc_grouped[0][:, :, t], by_block[1][:, :, 0], by_block[2][:, :, 0], ADD)
                nc.vector.tensor_tensor(by_block[0][:, :, 1:], by_block[1][:, :, 1:], by_block[2][:, :, 1:], ADD)
        for s in range(1, PACK):
            nc.scalar.copy(wc_woven[s], wc_dealt[:, s])

        def quantise_wc(s, codes):
            plane = keep.tile([P, P], U8, name=f"wc_plane{s}", align_bytes=64)
            nc.vector.quantize_mx(codes.bitcast(FP8X4), plane[:], wc_grouped[s][:].rearrange("p m t -> p (m t)"))
            return codes, plane

        first_codes = keep.tile([P, P], U32, name="first_codes", align_bytes=64)
        wc_mx = [quantise_wc(0, first_codes[:])]

        slot_words = keep.tile([P, J], U32, name="slot_words", align_bytes=64)
        for lo, hi in runs(SLOT_PIECES):
            nc.vector.tensor_copy(slot_words[:, lo:hi], token_words[:].indirect(entries(list1, lo, hi)))

        other_codes = keep.tile([P, PACK - 1, P], U32, name="other_codes", tag="words", align_bytes=64)
        wc_mx.extend(quantise_wc(s, other_codes[:, s - 1, :]) for s in range(1, PACK))

        a_rows = []
        for s, (codes, plane) in enumerate(wc_mx):
            rows = keep.tile([P, J], F32, name=f"a_rows{s}")
            for lo, hi in runs(SLOT_PIECES if s == 0 else (BANK, BANK)):
                bank = psum.tile([P, BANK], F32, name="bank")
                nc.tensor.matmul_mx(
                    bank[:, : hi - lo],
                    lhsT=codes.bitcast(FP8X4),
                    lhsT_scale=plane[:],
                    rhs=slot_words[:, lo:hi].bitcast(FP8X4),
                    rhs_scale=slot_scales[:, lo:hi],
                    start=True,
                    stop=True,
                )
                if s == 0:
                    nc.scalar.copy(rows[:, lo:hi], bank[:, : hi - lo])
                else:
                    nc.vector.tensor_copy(rows[:, lo:hi], bank[:, : hi - lo])
            a_rows.append(rows)

        second = keep.tile([P, PACK, O], F32, name="second")
        for s in range(PACK):
            nc.scalar.activation(second[:, s, :], a_rows[s][:].indirect(list5[:]), COPY, scale=sb_col[:, s : s + 1])

        chunks = runs(PLACE_CHUNKS)
        last_lo = chunks[-2][0]
        early = [psum.tile([P, BANK], F32, name="bank") for n in range(N // P)]
        late = [psum.tile([P, BANK], F32, name="bank") for n in range(N // P)]
        for number, (lo, hi) in enumerate(chunks):
            width = hi - lo
            first = ring.tile([P, PACK, width], F32, name="first")
            for s in range(PACK):
                nc.scalar.activation(
                    first[:, s, :], a_rows[s][:].indirect(entries(list4, lo, hi)), COPY, scale=sa_col[:, s : s + 1]
                )
            grouped = keep.tile([P, width, PACK], BF16, name=f"hid_grouped{number}", tag=f"hid{number}", align_bytes=64)
            if number < 2:
                larger = keep.tile([P, PACK, width], BF16, name=f"larger{number}")
                for rows in (slice(0, last), slice(last, PACK)):
                    nc.vector.tensor_tensor(larger[:, rows, :], first[:, rows, :], second[:, rows, lo:hi], MAX)
                nc.vector.tensor_copy(
                    grouped[:].rearrange("p (c i) s -> p c s i", i=4), larger[:].rearrange("p s (c i) -> p c s i", i=4)
                )
            else:
                nc.vector.tensor_tensor(
                    grouped[:].rearrange("p (c i) s -> p c s i", i=2),
                    first[:].rearrange("p s (c i) -> p c s i", i=2),
                    second[:, :, lo:hi].rearrange("p s (c i) -> p c s i", i=2),
                    MAX,
                )
            codes = keep.tile([P, width], U32, name=f"hid_codes{number}", align_bytes=64)
            plane = keep.tile([P, width], U8, name=f"hid_plane{number}", align_bytes=64)
            nc.vector.quantize_mx(codes[:].bitcast(FP8X4), plane[:], grouped[:].rearrange("p o s -> p (o s)"))
            for n in range(N // P):
                target = late[n][:, lo - last_lo : hi - last_lo] if lo >= last_lo else early[n][:, lo:hi]
                nc.tensor.matmul_mx(
                    target,
                    lhsT=wb_codes[:, n * P : (n + 1) * P].bitcast(FP8X4),
                    lhsT_scale=wb_plane[:, n * P : (n + 1) * P],
                    rhs=codes[:].bitcast(FP8X4),
                    rhs_scale=plane[:],
                    start=True,
                    stop=True,
                )

        p_rows = [
            keep.tile([P, O], F32, name="p_rows0"),
            keep.tile([P, O], F32, name="p_rows1", tag=f"hid{len(chunks) - 1}", align_bytes=64),
        ]
        for n in range(N // P):
            empty = nc.scalar.copy if n == 0 else nc.vector.tensor_copy
            empty(p_rows[n][:, :last_lo], early[n][:, :last_lo])
            empty(p_rows[n][:, last_lo:], late[n][:, : O - last_lo])
            ends = keep.tile([P, U], F32, name=f"ends{n}")
            nc.scalar.activation(ends[:], p_rows[n][:].indirect(list6[:]), COPY, scale=so_col[:, n : n + 1])
            nc.vector.tensor_copy(pages[n][:].indirect(list7[:]), ends[:])
            nc.sync.dma_start(out[n * P : (n + 1) * P, :], pages[n][:])
